import numpy as np
import ml_dtypes


def mxq(x, axis, fmt="e4m3"):
    dtype, down = {"e4m3": (ml_dtypes.float8_e4m3fn, 7), "e5m2": (ml_dtypes.float8_e5m2, 14)}[fmt]
    v = np.moveaxis(np.asarray(x, np.float32).astype(ml_dtypes.bfloat16).astype(np.float64), axis, -1)
    blocks = v.reshape(v.shape[:-1] + (-1, 32))
    amax = np.abs(blocks).max(-1, keepdims=True)
    byte = np.maximum(np.where(amax > 0, np.frexp(amax)[1] - 1 + 127, 0) - down, 1)
    scale = np.exp2(byte - 127.0)
    codes = (blocks / scale).astype(np.float32).astype(dtype).astype(np.float64)
    return np.moveaxis((codes * scale).reshape(v.shape), -1, axis)


WIDE = False


def mx_kscale(k):
    if not WIDE:
        return np.ones(k)
    levels = np.array([10, -10, 5, -5, 0])
    if k % 512:
        return np.exp2(np.random.permutation(np.resize(levels, k // 32))).repeat(32)
    a = np.empty((k // 512, 16))
    for p in range(k // 512):
        a[p, :8] = np.random.permutation(np.resize(levels, 8))
        for g in range(8):
            far = levels[np.abs(levels - a[p, g]) >= 10]
            a[p, g + 8] = far[np.random.randint(len(far))]
    return np.exp2(a.ravel()).repeat(32)


def f64(x):
    return np.asarray(x).astype(np.float64)


def striped(idx):
    return np.tile(np.asarray(idx).reshape(-1, 16).T, (8, 1)).astype(np.uint16)


def unstriped(offs):
    return offs[:16].T.reshape(-1).astype(np.int64)


def striped8(idx):
    return np.asarray(idx).reshape(8, -1, 16).transpose(0, 2, 1).reshape(128, -1).astype(np.uint16)


def unstriped8(offs):
    return offs.reshape(8, 16, -1).transpose(0, 2, 1).reshape(8, -1).astype(np.int64)


def pick8(x, idx, run):
    r = np.arange(len(x))
    return x[r[:, None], idx[r % (8 * run) // run]]


E2M1 = np.array([0.0, 0.5, 1.0, 1.5, 2.0, 3.0, 4.0, 6.0, -0.0, -0.5, -1.0, -1.5, -2.0, -3.0, -4.0, -6.0])


def pack_weight(w, fmt):
    k, n = w.shape
    w = f64(np.asarray(w, np.float32).astype(ml_dtypes.bfloat16)).reshape(k // 32, 32, n)
    amax = np.abs(w).max(1)
    if fmt == "e4m3":
        byte = np.frexp(amax)[1] - 1 + 127 - 7
    else:
        mant, ex = np.frexp(amax / 6.0)
        byte = np.where(mant > 0.5, ex, ex - 1) + 127
    byte = np.clip(np.where(amax > 0, byte, 1), 1, 254)
    scaled = (w * np.exp2(127.0 - byte)[:, None, :]).reshape(k, n).astype(np.float32)
    by_word = np.ascontiguousarray(scaled.reshape(k // 512, 128, 4, n).transpose(0, 1, 3, 2))
    if fmt == "e4m3":
        words = by_word.astype(ml_dtypes.float8_e4m3fn).view(np.uint8)
    else:
        c = by_word.astype(ml_dtypes.float4_e2m1fn).view(np.uint8) & 0xF
        words = (c[..., 0::2] | (c[..., 1::2] << 4)).reshape(k // 512, 128, 2 * n)
    return np.ascontiguousarray(words), np.ascontiguousarray(byte.astype(np.uint8).reshape(k // 512, 16, n))


def unpack_weight(words, scales, fmt):
    g, _, n = scales.shape
    words = np.ascontiguousarray(words).reshape(g, 128, n, -1)
    if fmt == "e4m3":
        vals = words.view(ml_dtypes.float8_e4m3fn).astype(np.float64)
    else:
        nib = np.empty((g, 128, n, 4), np.uint8)
        nib[..., 0::2] = words & 0xF
        nib[..., 1::2] = words >> 4
        vals = E2M1[nib]
    vals = vals * np.repeat(np.exp2(scales.astype(np.float64) - 127.0), 8, axis=1)[..., None]
    return vals.transpose(0, 1, 3, 2).reshape(g * 512, n)


K, J, R, T, Z, M, O, C, D, N, S = 512, 256, 512, 1024, 512, 1024, 128, 512, 512, 256, 1024


def setup_inputs():
    n = np.random.standard_normal
    idx = np.random.permutation(T)[:J]
    idx2 = np.random.permutation(M)[:J]
    idx3 = np.stack([np.random.permutation(C)[:J] for _ in range(8)])
    idx4 = np.stack([np.random.permutation(C)[:J] for _ in range(8)])
    idx5 = np.stack([np.random.permutation(D)[:J] for _ in range(8)])
    idx6 = np.stack([np.random.permutation(D)[:O] for _ in range(8)])
    idx7 = np.random.permutation(S)[:N]
    fk = mx_kscale(K)
    fr = mx_kscale(R)
    fz = mx_kscale(Z)
    xtp = pack_weight(n((K, T)) * fk[:, None], "e4m3")
    wp = pack_weight(n((K, R)) * 1 / np.sqrt(K) / fk[:, None] * fr, "e4m3")
    xop = pack_weight(n((Z, M)) / fz[:, None], "e4m3")
    w2p = pack_weight(n((Z, R)) * 1 / np.sqrt(Z) * fz[:, None] * fr, "e2m1")
    vsp = pack_weight(n((R, S)) * 1 / np.sqrt(R) / fr[:, None], "e2m1")
    return {
        "xt_words": xtp[0],
        "xt_scales": xtp[1],
        "w_words": wp[0],
        "w_scales": wp[1],
        "xo_words": xop[0],
        "xo_scales": xop[1],
        "w2_words": w2p[0],
        "w2_scales": w2p[1],
        "sa": (np.random.uniform(0.5, 1.6, (R, 1))).astype(np.float32),
        "sb": (np.random.uniform(0.5, 1.6, (R, 1))).astype(np.float32),
        "vs_words": vsp[0],
        "vs_scales": vsp[1],
        "offs": striped(idx),
        "offs2": striped(idx2),
        "offs3": striped8(idx3),
        "offs4": striped8(idx4),
        "offs5": striped8(idx5),
        "offs6": striped8(idx6),
        "offs7": striped(idx7),
    }


def reference(xt_words, xt_scales, w_words, w_scales, xo_words, xo_scales, w2_words, w2_scales, sa, sb, vs_words, vs_scales, offs, offs2, offs3, offs4, offs5, offs6, offs7):
    idx = unstriped(offs)
    idx2 = unstriped(offs2)
    idx3 = unstriped8(offs3)
    idx4 = unstriped8(offs4)
    idx5 = unstriped8(offs5)
    idx6 = unstriped8(offs6)
    idx7 = unstriped(offs7)
    xtu = unpack_weight(xt_words, xt_scales, "e4m3")
    wu = unpack_weight(w_words, w_scales, "e4m3")
    xou = unpack_weight(xo_words, xo_scales, "e4m3")
    w2u = unpack_weight(w2_words, w2_scales, "e2m1")
    vsu = unpack_weight(vs_words, vs_scales, "e2m1")
    xtidxg = xtu[:, idx]
    a = wu.T @ xtidxg
    xoidx2g = xou[:, idx2]
    b = w2u.T @ xoidx2g
    pw = np.zeros((R, C))
    pw[np.arange(R)[:, None], idx3[np.arange(R) % 512 // 64]] = a
    h1 = b - pick8(pw, idx4, 64) * f64(sa)
    pv = np.zeros((R, D))
    pv[np.arange(R)[:, None], idx5[np.arange(R) % 512 // 64]] = h1
    g1 = np.maximum(pv, 0.0)
    hid = pick8(g1, idx6, 64) * f64(sb)
    vsidx7g = vsu[:, idx7]
    hidq = mxq(hid, 0, "e4m3")
    y = vsidx7g.T @ hidq
    return y

@@ -1,0 +1,203 @@
+from contextlib import ExitStack
+
+import concourse.mybir as mybir
+
+K, J, R, T, O, C, N = 512, 256, 512, 1024, 128, 512, 256
+FLOPS = 2 * K * R * J * 2 + 2 * R * N * O
+
+F32 = mybir.dt.float32
+BF16 = mybir.dt.bfloat16
+I32 = mybir.dt.int32
+U32 = mybir.dt.uint32
+U16 = mybir.dt.uint16
+U8 = mybir.dt.uint8
+FP8X4 = mybir.dt.float8_e4m3fn_x4
+FP4X4 = mybir.dt.float4_e2m1fn_x4
+COPY = mybir.ActivationFunctionType.Copy
+SUB = mybir.AluOpType.subtract
+
+P = 128
+PACK = 4
+QUADS = 4
+
+
+def tile_picked_tokens_plain_two_deltapost_store_plain_kernel(
+    tc, xt_words, xt_scales, w_words, w_scales, xo_words, xo_scales, w2_words, w2_scales,
+    sa, sb, vs_words, vs_scales, offs, offs2, offs3, offs4, offs5, offs6, offs7, out,
+):
+    nc = tc.nc
+    with ExitStack() as ctx:
+        keep = ctx.enter_context(tc.tile_pool(name="keep", bufs=1))
+        psum = ctx.enter_context(tc.psum_pool(name="psum", bufs=1))
+
+        def load_list(src, name):
+            dst = keep.tile(list(src.shape), U16, name=name)
+            nc.sync.dma_start(dst[:], src)
+            return dst
+
+        def load_words8(src, name, tag):
+            dst = keep.tile([P, src.shape[2]], I32, name=name, tag=tag, align_bytes=64)
+            nc.sync.dma_start(dst[:], src[0].rearrange("p n t -> p (n t)").bitcast(I32))
+            return dst
+
+        def load_words4(src, dtype, width, name, tag):
+            dst = keep.tile([P, width], dtype, name=name, tag=tag, align_bytes=64)
+            nc.sync.dma_start(dst[:].bitcast(I32), src[0].bitcast(I32))
+            return dst
+
+        def zeroed_plane(width, name, tag):
+            dst = keep.tile([P, width], U8, name=name, tag=tag, align_bytes=64)
+            nc.vector.memset(dst[:].bitcast(I32), 0)
+            return dst
+
+        def load_scales(dst, src):
+            for q in range(QUADS):
+                nc.sync.dma_start(dst[32 * q : 32 * q + 4, :].bitcast(I32), src[0, 4 * q : 4 * q + 4, :].bitcast(I32))
+
+        xt_plane = zeroed_plane(T, "xt_plane", "table_plane")
+        w_plane = zeroed_plane(R, "w_plane", "matrix_plane")
+        pw = [keep.tile([P, C], F32, name="pw%d" % t, tag="board%d" % t) for t in range(PACK)]
+        pv = []
+        for board in pw:
+            nc.vector.memset(board[:], 0.0)
+
+        w_rows = keep.tile([4, QUADS, R], U8, name="w_rows", align_bytes=64)
+        nc.sync.dma_start(w_rows[:].bitcast(I32), w_scales[0].rearrange("(q j) n -> j q n", j=4).bitcast(I32))
+        list1 = load_list(offs, "list1")
+        xt_all = load_words8(xt_words, "xt_all", "table_words")
+        load_scales(xt_plane, xt_scales)
+        w_raw = load_words8(w_words, "w_raw", "matrix_words")
+        list3 = load_list(offs3, "list3")
+        list4 = load_list(offs4, "list4")
+        list2 = load_list(offs2, "list2")
+        list5 = load_list(offs5, "list5")
+        list6 = load_list(offs6, "list6")
+        list7 = load_list(offs7, "list7")
+        sa_sb = keep.tile([P, PACK], F32, name="sa_sb")
+        nc.gpsimd.dma_start(sa_sb[:], sa.rearrange("(p t) o -> p (t o)", t=PACK))
+        sb_sb = keep.tile([P, PACK], F32, name="sb_sb")
+        nc.gpsimd.dma_start(sb_sb[:], sb.rearrange("(p t) o -> p (t o)", t=PACK))
+
+        def gather(window, lst, dtype, width, name):
+            dst = keep.tile([P, width], dtype, name=name, tag=name, align_bytes=64)
+            nc.vector.tensor_copy(dst[:], window.indirect(lst[:]))
+            return dst
+
+        def deal_plane(plane, t, name):
+            part = keep.tile([P, P], U8, name="%s%d" % (name, t), align_bytes=64)
+            nc.vector.tensor_copy(part[:], plane[:, t::PACK])
+            return part
+
+        w_dealt = keep.tile([P, R], U32, name="w_dealt", align_bytes=64)
+        nc.scalar.copy(
+            w_dealt[:].rearrange("p (t m) -> p m t", t=PACK),
+            w_raw[:].bitcast(U32).rearrange("p (m t) -> p m t", t=PACK),
+        )
+        for q in range(QUADS):
+            nc.vector.tensor_copy(w_plane[32 * q : 32 * q + 4, :].bitcast(I32), w_rows[:, q, :].bitcast(I32))
+        w_first_scales = deal_plane(w_plane, 0, "w_first_scales")
+        xt_picked = gather(xt_all[:].bitcast(U32), list1, U32, J, "xt_picked")
+        xt_picked_scales = gather(xt_plane[:], list1, U8, J, "xt_picked_scales")
+        w_rest_scales = keep.tile([P, PACK - 1, P], U8, name="w_rest_scales", tag="table_plane", align_bytes=64)
+        nc.vector.tensor_copy(
+            w_rest_scales[:].rearrange("p t m -> p m t"), w_plane[:].rearrange("p (m t) -> p m t", t=PACK)[:, :, 1:]
+        )
+        w_dealt_scales = [w_first_scales[:]] + [w_rest_scales[:, t, :] for t in range(PACK - 1)]
+        a_sb = []
+        for t in range(PACK):
+            a_ps = psum.tile([P, J], F32, name="a_ps%d" % t, tag="a_ps%d" % t)
+            nc.tensor.matmul_mx(
+                out=a_ps[:], lhsT=w_dealt[:, t * P : (t + 1) * P].bitcast(FP8X4), lhsT_scale=w_dealt_scales[t],
+                rhs=xt_picked[:].bitcast(FP8X4), rhs_scale=xt_picked_scales[:], start=True, stop=True,
+            )
+            a_t = keep.tile([P, J], F32, name="a_sb%d" % t)
+            nc.vector.tensor_copy(a_t[:], a_ps[:])
+            a_sb.append(a_t)
+
+        xo_all = load_words8(xo_words, "xo_all", "table_words")
+        xo_plane = zeroed_plane(T, "xo_plane", "table_plane")
+        load_scales(xo_plane, xo_scales)
+        w2_raw = load_words4(w2_words, U8, 2 * R, "w2_raw", "matrix_words")
+        w2_plane = zeroed_plane(R, "w2_plane", "matrix_plane")
+        load_scales(w2_plane, w2_scales)
+        xo_picked = gather(xo_all[:].bitcast(U32), list2, U32, J, "xo_picked")
+        xo_picked_scales = gather(xo_plane[:], list2, U8, J, "xo_picked_scales")
+        w2_dealt = keep.tile([P, 2 * R], U8, name="w2_dealt", align_bytes=64)
+        nc.vector.tensor_copy(
+            w2_dealt[:].rearrange("p (t m b) -> p m t b", t=PACK, b=2),
+            w2_raw[:].rearrange("p (m t b) -> p m t b", t=PACK, b=2),
+        )
+        w2_dealt_scales = keep.tile([P, PACK, P], U8, name="w2_dealt_scales", align_bytes=64)
+        nc.vector.tensor_copy(
+            w2_dealt_scales[:].rearrange("p t m -> p m t"), w2_plane[:].rearrange("p (m t) -> p m t", t=PACK)
+        )
+        b_ps = []
+        for t in range(PACK):
+            b_t = psum.tile([P, J], F32, name="b_ps%d" % t)
+            nc.tensor.matmul_mx(
+                out=b_t[:], lhsT=w2_dealt[:, 2 * t * P : 2 * (t + 1) * P].bitcast(FP4X4), lhsT_scale=w2_dealt_scales[:, t, :],
+                rhs=xo_picked[:].bitcast(FP8X4), rhs_scale=xo_picked_scales[:], start=True, stop=True,
+            )
+            b_ps.append(b_t)
+
+        vs_all = load_words4(vs_words, U16, T, "vs_all", "table_words")
+        vs_plane = zeroed_plane(T, "vs_plane", "table_plane")
+        load_scales(vs_plane, vs_scales)
+        vs_picked = gather(vs_all[:], list7, U16, N, "vs_picked")
+        vs_picked_scales = gather(vs_plane[:], list7, U8, N, "vs_picked_scales")
+
+        taken = keep.tile([P, PACK, J], F32, name="taken", tag="xt_picked", align_bytes=64)
+        kept = [keep.tile([P, J], F32, name="kept%d" % t) for t in range(PACK)]
+
+        def put_a(t):
+            nc.scalar.activation(out=pw[t][:].indirect(list3[:]), in_=a_sb[t][:], func=COPY)
+
+        def fetch_pw(t):
+            nc.scalar.activation(out=taken[:, t, :], in_=pw[t][:].indirect(list4[:]), func=COPY, scale=sa_sb[:, t : t + 1])
+            h1 = keep.tile([P, J], F32, name="h1_%d" % t, tag="h1_%d" % t, align_bytes=64)
+            nc.vector.tensor_tensor(h1[:], b_ps[t][:], taken[:, t, :], SUB)
+            nc.vector.tensor_scalar_max(kept[t][:], h1[:], 0.0)
+            board = keep.tile([P, C], F32, name="pv%d" % t, tag="board%d" % t)
+            nc.gpsimd.memset(board[:], 0.0)
+            pv.append(board)
+
+        def put_h(t):
+            nc.scalar.activation(out=pv[t][:].indirect(list5[:]), in_=kept[t][:], func=COPY)
+
+        def fetch_g(t):
+            nc.scalar.activation(out=hid[:, t, :], in_=pv[t][:].indirect(list6[:]), func=COPY, scale=sb_sb[:, t : t + 1])
+
+        for t in range(PACK):
+            put_a(t)
+        for t in range(PACK):
+            fetch_pw(t)
+        for t in range(PACK):
+            put_h(t)
+        hid = keep.tile([P, PACK, O], BF16, name="hid", tag="h1_%d" % (PACK - 1), align_bytes=64)
+        for t in range(PACK):
+            fetch_g(t)
+
+        woven = keep.tile([P, O, PACK], BF16, name="woven", align_bytes=64)
+        nc.vector.tensor_copy(
+            woven[:].rearrange("p (c i) t -> p c t i", i=4),
+            hid[:].rearrange("p t (c i) -> p c t i", i=4),
+        )
+        hid_codes = keep.tile([P, O], U32, name="hid_codes", align_bytes=64)
+        hid_scales = keep.tile([P, O], U8, name="hid_scales", align_bytes=64)
+        nc.vector.quantize_mx(
+            out=hid_codes[:].bitcast(FP8X4), scales=hid_scales[:], in_=woven[:].rearrange("p o t -> p (o t)"),
+        )
+        for half in range(N // P):
+            y_ps = psum.tile([P, O], F32, name="y_ps%d" % half, tag="a_ps%d" % half)
+            nc.tensor.matmul_mx(
+                out=y_ps[:], lhsT=vs_picked[:, half * P : (half + 1) * P].bitcast(FP4X4),
+                lhsT_scale=vs_picked_scales[:, half * P : (half + 1) * P],
+                rhs=hid_codes[:].bitcast(FP8X4), rhs_scale=hid_scales[:], start=True, stop=True,
+            )
+            y_sb = keep.tile([P, O], F32, name="y_sb%d" % half)
+            if half == 0:
+                nc.vector.tensor_copy(y_sb[:], y_ps[:])
+                nc.sync.dma_start(out[half * P : (half + 1) * P, :], y_sb[:])
+            else:
+                nc.scalar.copy(y_sb[:], y_ps[:])
+                nc.scalar.dma_start(out[half * P : (half + 1) * P, :], y_sb[:])

@@ -56,20 +56,25 @@ def tile_picked_tokens_plain_two_deltapost_store_plain_kernel(
 
         xt_plane = zeroed_plane(T, "xt_plane", "table_plane")
         w_plane = zeroed_plane(R, "w_plane", "matrix_plane")
-        pw = [keep.tile([P, C], F32, name="pw%d" % t, tag="board%d" % t) for t in range(PACK)]
-        pv = []
+        pw = [keep.tile([P, C], F32, name="pw%d" % t) for t in range(PACK - 1)]
         for board in pw:
             nc.vector.memset(board[:], 0.0)
 
         w_rows = keep.tile([4, QUADS, R], U8, name="w_rows", align_bytes=64)
-        nc.sync.dma_start(w_rows[:].bitcast(I32), w_scales[0].rearrange("(q j) n -> j q n", j=4).bitcast(I32))
+        nc.scalar.dma_start(w_rows[:].bitcast(I32), w_scales[0].rearrange("(q j) n -> j q n", j=4).bitcast(I32))
         list1 = load_list(offs, "list1")
         xt_all = load_words8(xt_words, "xt_all", "table_words")
         load_scales(xt_plane, xt_scales)
         w_raw = load_words8(w_words, "w_raw", "matrix_words")
         list3 = load_list(offs3, "list3")
-        list4 = load_list(offs4, "list4")
         list2 = load_list(offs2, "list2")
+        xo_all = load_words8(xo_words, "xo_all", "xo_all")
+        w2_raw = load_words4(w2_words, U8, 2 * R, "w2_raw", "w2_raw")
+        xo_plane = zeroed_plane(T, "xo_plane", "xo_plane")
+        load_scales(xo_plane, xo_scales)
+        w2_plane = zeroed_plane(R, "w2_plane", "w2_plane")
+        load_scales(w2_plane, w2_scales)
+        list4 = load_list(offs4, "list4")
         list5 = load_list(offs5, "list5")
         list6 = load_list(offs6, "list6")
         list7 = load_list(offs7, "list7")
@@ -78,17 +83,17 @@ def tile_picked_tokens_plain_two_deltapost_store_plain_kernel(
         sb_sb = keep.tile([P, PACK], F32, name="sb_sb")
         nc.gpsimd.dma_start(sb_sb[:], sb.rearrange("(p t) o -> p (t o)", t=PACK))
 
-        def gather(window, lst, dtype, width, name):
-            dst = keep.tile([P, width], dtype, name=name, tag=name, align_bytes=64)
+        def gather(window, lst, dtype, width, name, tag):
+            dst = keep.tile([P, width], dtype, name=name, tag=tag, align_bytes=64)
             nc.vector.tensor_copy(dst[:], window.indirect(lst[:]))
             return dst
 
         def deal_plane(plane, t, name):
-            part = keep.tile([P, P], U8, name="%s%d" % (name, t), align_bytes=64)
+            part = keep.tile([P, P], U8, name=name, tag=name, align_bytes=64)
             nc.vector.tensor_copy(part[:], plane[:, t::PACK])
             return part
 
-        w_dealt = keep.tile([P, R], U32, name="w_dealt", align_bytes=64)
+        w_dealt = keep.tile([P, R], U32, name="w_dealt", tag="dealt_words", align_bytes=64)
         nc.scalar.copy(
             w_dealt[:].rearrange("p (t m) -> p m t", t=PACK),
             w_raw[:].bitcast(U32).rearrange("p (m t) -> p m t", t=PACK),
@@ -96,8 +101,8 @@ def tile_picked_tokens_plain_two_deltapost_store_plain_kernel(
         for q in range(QUADS):
             nc.vector.tensor_copy(w_plane[32 * q : 32 * q + 4, :].bitcast(I32), w_rows[:, q, :].bitcast(I32))
         w_first_scales = deal_plane(w_plane, 0, "w_first_scales")
-        xt_picked = gather(xt_all[:].bitcast(U32), list1, U32, J, "xt_picked")
-        xt_picked_scales = gather(xt_plane[:], list1, U8, J, "xt_picked_scales")
+        xt_picked = gather(xt_all[:].bitcast(U32), list1, U32, J, "xt_picked", "picked_words")
+        xt_picked_scales = gather(xt_plane[:], list1, U8, J, "xt_picked_scales", "picked_scales")
         w_rest_scales = keep.tile([P, PACK - 1, P], U8, name="w_rest_scales", tag="table_plane", align_bytes=64)
         nc.vector.tensor_copy(
             w_rest_scales[:].rearrange("p t m -> p m t"), w_plane[:].rearrange("p (m t) -> p m t", t=PACK)[:, :, 1:]
@@ -114,20 +119,18 @@ def tile_picked_tokens_plain_two_deltapost_store_plain_kernel(
             nc.vector.tensor_copy(a_t[:], a_ps[:])
             a_sb.append(a_t)
 
-        xo_all = load_words8(xo_words, "xo_all", "table_words")
-        xo_plane = zeroed_plane(T, "xo_plane", "table_plane")
-        load_scales(xo_plane, xo_scales)
-        w2_raw = load_words4(w2_words, U8, 2 * R, "w2_raw", "matrix_words")
-        w2_plane = zeroed_plane(R, "w2_plane", "matrix_plane")
-        load_scales(w2_plane, w2_scales)
-        xo_picked = gather(xo_all[:].bitcast(U32), list2, U32, J, "xo_picked")
-        xo_picked_scales = gather(xo_plane[:], list2, U8, J, "xo_picked_scales")
-        w2_dealt = keep.tile([P, 2 * R], U8, name="w2_dealt", align_bytes=64)
+        last_board = keep.tile([P, C], F32, name="pw3", tag="matrix_plane", align_bytes=64)
+        nc.vector.memset(last_board[:], 0.0)
+        pw.append(last_board)
+
+        xo_picked = gather(xo_all[:].bitcast(U32), list2, U32, J, "xo_picked", "picked_words")
+        xo_picked_scales = gather(xo_plane[:], list2, U8, J, "xo_picked_scales", "picked_scales")
+        w2_dealt = keep.tile([P, 2 * R], U8, name="w2_dealt", tag="dealt_words", align_bytes=64)
         nc.vector.tensor_copy(
             w2_dealt[:].rearrange("p (t m b) -> p m t b", t=PACK, b=2),
             w2_raw[:].rearrange("p (m t b) -> p m t b", t=PACK, b=2),
         )
-        w2_dealt_scales = keep.tile([P, PACK, P], U8, name="w2_dealt_scales", align_bytes=64)
+        w2_dealt_scales = keep.tile([P, PACK, P], U8, name="w2_dealt_scales", tag="table_plane", align_bytes=64)
         nc.vector.tensor_copy(
             w2_dealt_scales[:].rearrange("p t m -> p m t"), w2_plane[:].rearrange("p (m t) -> p m t", t=PACK)
         )
@@ -140,13 +143,16 @@ def tile_picked_tokens_plain_two_deltapost_store_plain_kernel(
             )
             b_ps.append(b_t)
 
-        vs_all = load_words4(vs_words, U16, T, "vs_all", "table_words")
-        vs_plane = zeroed_plane(T, "vs_plane", "table_plane")
-        load_scales(vs_plane, vs_scales)
-        vs_picked = gather(vs_all[:], list7, U16, N, "vs_picked")
-        vs_picked_scales = gather(vs_plane[:], list7, U8, N, "vs_picked_scales")
+        spent = ("xo_all", "w2_raw", "w2_plane", "dealt_words")
+        pv = [keep.tile([P, C], F32, name="pv%d" % t, tag=spent[t], align_bytes=64) for t in range(PACK)]
+        for board in pv:
+            nc.vector.memset(board[:], 0.0)
 
-        taken = keep.tile([P, PACK, J], F32, name="taken", tag="xt_picked", align_bytes=64)
+        vs_all = load_words4(vs_words, U16, T, "vs_all", "table_words")
+        vs_plane = zeroed_plane(T, "vs_plane", "w_first_scales")
+        load_scales(vs_plane, vs_scales)
+
+        taken = keep.tile([P, PACK, J], F32, name="taken", tag="xo_plane", align_bytes=64)
         kept = [keep.tile([P, J], F32, name="kept%d" % t) for t in range(PACK)]
 
         def put_a(t):
@@ -157,9 +163,6 @@ def tile_picked_tokens_plain_two_deltapost_store_plain_kernel(
             h1 = keep.tile([P, J], F32, name="h1_%d" % t, tag="h1_%d" % t, align_bytes=64)
             nc.vector.tensor_tensor(h1[:], b_ps[t][:], taken[:, t, :], SUB)
             nc.vector.tensor_scalar_max(kept[t][:], h1[:], 0.0)
-            board = keep.tile([P, C], F32, name="pv%d" % t, tag="board%d" % t)
-            nc.gpsimd.memset(board[:], 0.0)
-            pv.append(board)
 
         def put_h(t):
             nc.scalar.activation(out=pv[t][:].indirect(list5[:]), in_=kept[t][:], func=COPY)
@@ -171,6 +174,8 @@ def tile_picked_tokens_plain_two_deltapost_store_plain_kernel(
             put_a(t)
         for t in range(PACK):
             fetch_pw(t)
+        vs_picked = gather(vs_all[:], list7, U16, N, "vs_picked", "h1_0")
+        vs_picked_scales = gather(vs_plane[:], list7, U8, N, "vs_picked_scales", "h1_1")
         for t in range(PACK):
             put_h(t)
         hid = keep.tile([P, PACK, O], BF16, name="hid", tag="h1_%d" % (PACK - 1), align_bytes=64)

@@ -19,6 +19,7 @@ SUB = mybir.AluOpType.subtract
 P = 128
 PACK = 4
 QUADS = 4
+HALF = J // 2
 
 
 def tile_picked_tokens_plain_two_deltapost_store_plain_kernel(
@@ -51,12 +52,12 @@ def tile_picked_tokens_plain_two_deltapost_store_plain_kernel(
             return dst
 
         def load_scales(dst, src):
-            for q in range(QUADS):
-                nc.sync.dma_start(dst[32 * q : 32 * q + 4, :].bitcast(I32), src[0, 4 * q : 4 * q + 4, :].bitcast(I32))
+            for j in range(4):
+                nc.sync.dma_start(dst[j::32, :].bitcast(I32), src[0, j::4, :].bitcast(I32))
 
         xt_plane = zeroed_plane(T, "xt_plane", "table_plane")
         w_plane = zeroed_plane(R, "w_plane", "matrix_plane")
-        pw = [keep.tile([P, C], F32, name="pw%d" % t) for t in range(PACK - 1)]
+        pw = [keep.tile([P, C], F32, name="pw%d" % t, tag="pw%d" % t) for t in range(2)]
         for board in pw:
             nc.vector.memset(board[:], 0.0)
 
@@ -79,9 +80,9 @@ def tile_picked_tokens_plain_two_deltapost_store_plain_kernel(
         list6 = load_list(offs6, "list6")
         list7 = load_list(offs7, "list7")
         sa_sb = keep.tile([P, PACK], F32, name="sa_sb")
-        nc.gpsimd.dma_start(sa_sb[:], sa.rearrange("(p t) o -> p (t o)", t=PACK))
+        nc.sync.dma_start(sa_sb[:], sa.rearrange("(p t) o -> p (t o)", t=PACK))
         sb_sb = keep.tile([P, PACK], F32, name="sb_sb")
-        nc.gpsimd.dma_start(sb_sb[:], sb.rearrange("(p t) o -> p (t o)", t=PACK))
+        nc.sync.dma_start(sb_sb[:], sb.rearrange("(p t) o -> p (t o)", t=PACK))
 
         def gather(window, lst, dtype, width, name, tag):
             dst = keep.tile([P, width], dtype, name=name, tag=tag, align_bytes=64)
@@ -89,15 +90,15 @@ def tile_picked_tokens_plain_two_deltapost_store_plain_kernel(
             return dst
 
         def deal_plane(plane, t, name):
-            part = keep.tile([P, P], U8, name=name, tag=name, align_bytes=64)
+            part = keep.tile([P, P], U8, name="%s%d" % (name, t), align_bytes=64)
             nc.vector.tensor_copy(part[:], plane[:, t::PACK])
             return part
 
-        w_dealt = keep.tile([P, R], U32, name="w_dealt", tag="dealt_words", align_bytes=64)
-        nc.scalar.copy(
-            w_dealt[:].rearrange("p (t m) -> p m t", t=PACK),
-            w_raw[:].bitcast(U32).rearrange("p (m t) -> p m t", t=PACK),
-        )
+        w_dealt = []
+        for t in range(PACK):
+            part = keep.tile([P, P], U32, name="w_dealt%d" % t, tag="w_dealt%d" % t, align_bytes=64)
+            nc.scalar.copy(part[:], w_raw[:].bitcast(U32)[:, t::PACK])
+            w_dealt.append(part)
         for q in range(QUADS):
             nc.vector.tensor_copy(w_plane[32 * q : 32 * q + 4, :].bitcast(I32), w_rows[:, q, :].bitcast(I32))
         w_first_scales = deal_plane(w_plane, 0, "w_first_scales")
@@ -108,24 +109,36 @@ def tile_picked_tokens_plain_two_deltapost_store_plain_kernel(
             w_rest_scales[:].rearrange("p t m -> p m t"), w_plane[:].rearrange("p (m t) -> p m t", t=PACK)[:, :, 1:]
         )
         w_dealt_scales = [w_first_scales[:]] + [w_rest_scales[:, t, :] for t in range(PACK - 1)]
-        a_sb = []
-        for t in range(PACK):
+        a_sb = [keep.tile([P, J], F32, name="a_sb0")]
+        for half in range(2):
+            cols = slice(half * HALF, (half + 1) * HALF)
+            a_ps = psum.tile([P, HALF], F32, name="a_half%d" % half, tag=("a_ps0", "b_ps3")[half])
+            nc.tensor.matmul_mx(
+                out=a_ps[:], lhsT=w_dealt[0][:].bitcast(FP8X4), lhsT_scale=w_dealt_scales[0],
+                rhs=xt_picked[:, cols].bitcast(FP8X4), rhs_scale=xt_picked_scales[:, cols], start=True, stop=True,
+            )
+            if half == 0:
+                nc.scalar.copy(a_sb[0][:, cols], a_ps[:])
+            else:
+                nc.vector.tensor_copy(a_sb[0][:, cols], a_ps[:])
+        for t in range(1, PACK):
             a_ps = psum.tile([P, J], F32, name="a_ps%d" % t, tag="a_ps%d" % t)
             nc.tensor.matmul_mx(
-                out=a_ps[:], lhsT=w_dealt[:, t * P : (t + 1) * P].bitcast(FP8X4), lhsT_scale=w_dealt_scales[t],
+                out=a_ps[:], lhsT=w_dealt[t][:].bitcast(FP8X4), lhsT_scale=w_dealt_scales[t],
                 rhs=xt_picked[:].bitcast(FP8X4), rhs_scale=xt_picked_scales[:], start=True, stop=True,
             )
-            a_t = keep.tile([P, J], F32, name="a_sb%d" % t)
+            a_t = keep.tile([P, J], F32, name="a_sb%d" % t, tag="a_sb%d" % t, align_bytes=64)
             nc.vector.tensor_copy(a_t[:], a_ps[:])
             a_sb.append(a_t)
 
-        last_board = keep.tile([P, C], F32, name="pw3", tag="matrix_plane", align_bytes=64)
-        nc.vector.memset(last_board[:], 0.0)
-        pw.append(last_board)
+        for t in range(2, PACK):
+            board = keep.tile([P, C], F32, name="pw%d" % t, tag="w_dealt%d" % (t - 1), align_bytes=64)
+            nc.vector.memset(board[:], 0.0)
+            pw.append(board)
 
         xo_picked = gather(xo_all[:].bitcast(U32), list2, U32, J, "xo_picked", "picked_words")
         xo_picked_scales = gather(xo_plane[:], list2, U8, J, "xo_picked_scales", "picked_scales")
-        w2_dealt = keep.tile([P, 2 * R], U8, name="w2_dealt", tag="dealt_words", align_bytes=64)
+        w2_dealt = keep.tile([P, 2 * R], U8, name="w2_dealt", tag="w_dealt3", align_bytes=64)
         nc.vector.tensor_copy(
             w2_dealt[:].rearrange("p (t m b) -> p m t b", t=PACK, b=2),
             w2_raw[:].rearrange("p (m t b) -> p m t b", t=PACK, b=2),
@@ -136,20 +149,20 @@ def tile_picked_tokens_plain_two_deltapost_store_plain_kernel(
         )
         b_ps = []
         for t in range(PACK):
-            b_t = psum.tile([P, J], F32, name="b_ps%d" % t)
+            b_t = psum.tile([P, J], F32, name="b_ps%d" % t, tag="b_ps%d" % t)
             nc.tensor.matmul_mx(
                 out=b_t[:], lhsT=w2_dealt[:, 2 * t * P : 2 * (t + 1) * P].bitcast(FP4X4), lhsT_scale=w2_dealt_scales[:, t, :],
                 rhs=xo_picked[:].bitcast(FP8X4), rhs_scale=xo_picked_scales[:], start=True, stop=True,
             )
             b_ps.append(b_t)
 
-        spent = ("xo_all", "w2_raw", "w2_plane", "dealt_words")
-        pv = [keep.tile([P, C], F32, name="pv%d" % t, tag=spent[t], align_bytes=64) for t in range(PACK)]
+        spent = ("xo_all", "w2_raw")
+        pv = [keep.tile([P, C], F32, name="pv%d" % t, tag=spent[t], align_bytes=64) for t in range(2)]
         for board in pv:
             nc.vector.memset(board[:], 0.0)
 
         vs_all = load_words4(vs_words, U16, T, "vs_all", "table_words")
-        vs_plane = zeroed_plane(T, "vs_plane", "w_first_scales")
+        vs_plane = zeroed_plane(T, "vs_plane", "w2_plane")
         load_scales(vs_plane, vs_scales)
 
         taken = keep.tile([P, PACK, J], F32, name="taken", tag="xo_plane", align_bytes=64)
@@ -170,10 +183,19 @@ def tile_picked_tokens_plain_two_deltapost_store_plain_kernel(
         def fetch_g(t):
             nc.scalar.activation(out=hid[:, t, :], in_=pv[t][:].indirect(list6[:]), func=COPY, scale=sb_sb[:, t : t + 1])
 
-        for t in range(PACK):
+        for half in range(2):
+            nc.scalar.activation(
+                out=pw[0][:].indirect(list3[:, half * HALF // 16 : (half + 1) * HALF // 16]),
+                in_=a_sb[0][:, half * HALF : (half + 1) * HALF], func=COPY,
+            )
+        for t in range(1, PACK):
             put_a(t)
         for t in range(PACK):
             fetch_pw(t)
+        for t in range(2, PACK):
+            board = keep.tile([P, C], F32, name="pv%d" % t, tag="pw%d" % (t - 2))
+            nc.vector.memset(board[:], 0.0)
+            pv.append(board)
         vs_picked = gather(vs_all[:], list7, U16, N, "vs_picked", "h1_0")
         vs_picked_scales = gather(vs_plane[:], list7, U8, N, "vs_picked_scales", "h1_1")
         for t in range(PACK):

@@ -51,9 +51,9 @@ def tile_picked_tokens_plain_two_deltapost_store_plain_kernel(
             nc.vector.memset(dst[:].bitcast(I32), 0)
             return dst
 
-        def load_scales(dst, src):
+        def load_scales(dst, src, queue):
             for j in range(4):
-                nc.sync.dma_start(dst[j::32, :].bitcast(I32), src[0, j::4, :].bitcast(I32))
+                queue.dma_start(dst[j::32, :].bitcast(I32), src[0, j::4, :].bitcast(I32))
 
         xt_plane = zeroed_plane(T, "xt_plane", "table_plane")
         w_plane = zeroed_plane(R, "w_plane", "matrix_plane")
@@ -65,16 +65,16 @@ def tile_picked_tokens_plain_two_deltapost_store_plain_kernel(
         nc.scalar.dma_start(w_rows[:].bitcast(I32), w_scales[0].rearrange("(q j) n -> j q n", j=4).bitcast(I32))
         list1 = load_list(offs, "list1")
         xt_all = load_words8(xt_words, "xt_all", "table_words")
-        load_scales(xt_plane, xt_scales)
+        load_scales(xt_plane, xt_scales, nc.sync)
         w_raw = load_words8(w_words, "w_raw", "matrix_words")
         list3 = load_list(offs3, "list3")
         list2 = load_list(offs2, "list2")
         xo_all = load_words8(xo_words, "xo_all", "xo_all")
         w2_raw = load_words4(w2_words, U8, 2 * R, "w2_raw", "w2_raw")
         xo_plane = zeroed_plane(T, "xo_plane", "xo_plane")
-        load_scales(xo_plane, xo_scales)
+        load_scales(xo_plane, xo_scales, nc.sync)
         w2_plane = zeroed_plane(R, "w2_plane", "w2_plane")
-        load_scales(w2_plane, w2_scales)
+        load_scales(w2_plane, w2_scales, nc.gpsimd)
         list4 = load_list(offs4, "list4")
         list5 = load_list(offs5, "list5")
         list6 = load_list(offs6, "list6")
@@ -163,7 +163,7 @@ def tile_picked_tokens_plain_two_deltapost_store_plain_kernel(
 
         vs_all = load_words4(vs_words, U16, T, "vs_all", "table_words")
         vs_plane = zeroed_plane(T, "vs_plane", "w2_plane")
-        load_scales(vs_plane, vs_scales)
+        load_scales(vs_plane, vs_scales, nc.sync)
 
         taken = keep.tile([P, PACK, J], F32, name="taken", tag="xo_plane", align_bytes=64)
         kept = [keep.tile([P, J], F32, name="kept%d" % t) for t in range(PACK)]

from contextlib import ExitStack

import concourse.mybir as mybir

K, J, R, T, O, C, N = 512, 256, 512, 1024, 128, 512, 256
FLOPS = 2 * K * R * J * 2 + 2 * R * N * O

F32 = mybir.dt.float32
BF16 = mybir.dt.bfloat16
I32 = mybir.dt.int32
U32 = mybir.dt.uint32
U16 = mybir.dt.uint16
U8 = mybir.dt.uint8
FP8X4 = mybir.dt.float8_e4m3fn_x4
FP4X4 = mybir.dt.float4_e2m1fn_x4
COPY = mybir.ActivationFunctionType.Copy
SUB = mybir.AluOpType.subtract

P = 128
PACK = 4
QUADS = 4
HALF = J // 2


def tile_picked_tokens_plain_two_deltapost_store_plain_kernel(
    tc, xt_words, xt_scales, w_words, w_scales, xo_words, xo_scales, w2_words, w2_scales,
    sa, sb, vs_words, vs_scales, offs, offs2, offs3, offs4, offs5, offs6, offs7, out,
):
    nc = tc.nc
    with ExitStack() as ctx:
        keep = ctx.enter_context(tc.tile_pool(name="keep", bufs=1))
        psum = ctx.enter_context(tc.psum_pool(name="psum", bufs=1))

        def load_list(src, name):
            dst = keep.tile(list(src.shape), U16, name=name)
            nc.sync.dma_start(dst[:], src)
            return dst

        def load_words8(src, name, tag):
            dst = keep.tile([P, src.shape[2]], I32, name=name, tag=tag, align_bytes=64)
            nc.sync.dma_start(dst[:], src[0].rearrange("p n t -> p (n t)").bitcast(I32))
            return dst

        def load_words4(src, dtype, width, name, tag):
            dst = keep.tile([P, width], dtype, name=name, tag=tag, align_bytes=64)
            nc.sync.dma_start(dst[:].bitcast(I32), src[0].bitcast(I32))
            return dst

        def zeroed_plane(width, name, tag):
            dst = keep.tile([P, width], U8, name=name, tag=tag, align_bytes=64)
            nc.vector.memset(dst[:].bitcast(I32), 0)
            return dst

        def load_scales(dst, src, queue):
            for j in range(4):
                queue.dma_start(dst[j::32, :].bitcast(I32), src[0, j::4, :].bitcast(I32))

        xt_plane = zeroed_plane(T, "xt_plane", "table_plane")
        w_plane = zeroed_plane(R, "w_plane", "matrix_plane")
        pw = [keep.tile([P, C], F32, name="pw%d" % t, tag="pw%d" % t) for t in range(2)]
        for board in pw:
            nc.vector.memset(board[:], 0.0)

        w_rows = keep.tile([4, QUADS, R], U8, name="w_rows", align_bytes=64)
        nc.scalar.dma_start(w_rows[:].bitcast(I32), w_scales[0].rearrange("(q j) n -> j q n", j=4).bitcast(I32))
        list1 = load_list(offs, "list1")
        xt_all = load_words8(xt_words, "xt_all", "table_words")
        load_scales(xt_plane, xt_scales, nc.sync)
        w_raw = load_words8(w_words, "w_raw", "matrix_words")
        list3 = load_list(offs3, "list3")
        list2 = load_list(offs2, "list2")
        xo_all = load_words8(xo_words, "xo_all", "xo_all")
        w2_raw = load_words4(w2_words, U8, 2 * R, "w2_raw", "w2_raw")
        xo_plane = zeroed_plane(T, "xo_plane", "xo_plane")
        load_scales(xo_plane, xo_scales, nc.sync)
        w2_plane = zeroed_plane(R, "w2_plane", "w2_plane")
        load_scales(w2_plane, w2_scales, nc.gpsimd)
        list4 = load_list(offs4, "list4")
        list5 = load_list(offs5, "list5")
        list6 = load_list(offs6, "list6")
        list7 = load_list(offs7, "list7")
        sa_sb = keep.tile([P, PACK], F32, name="sa_sb")
        nc.sync.dma_start(sa_sb[:], sa.rearrange("(p t) o -> p (t o)", t=PACK))
        sb_sb = keep.tile([P, PACK], F32, name="sb_sb")
        nc.sync.dma_start(sb_sb[:], sb.rearrange("(p t) o -> p (t o)", t=PACK))

        def gather(window, lst, dtype, width, name, tag):
            dst = keep.tile([P, width], dtype, name=name, tag=tag, align_bytes=64)
            nc.vector.tensor_copy(dst[:], window.indirect(lst[:]))
            return dst

        def deal_plane(plane, t, name):
            part = keep.tile([P, P], U8, name="%s%d" % (name, t), align_bytes=64)
            nc.vector.tensor_copy(part[:], plane[:, t::PACK])
            return part

        w_dealt = []
        for t in range(PACK):
            part = keep.tile([P, P], U32, name="w_dealt%d" % t, tag="w_dealt%d" % t, align_bytes=64)
            nc.scalar.copy(part[:], w_raw[:].bitcast(U32)[:, t::PACK])
            w_dealt.append(part)
        for q in range(QUADS):
            nc.vector.tensor_copy(w_plane[32 * q : 32 * q + 4, :].bitcast(I32), w_rows[:, q, :].bitcast(I32))
        w_first_scales = deal_plane(w_plane, 0, "w_first_scales")
        xt_picked = gather(xt_all[:].bitcast(U32), list1, U32, J, "xt_picked", "picked_words")
        xt_picked_scales = gather(xt_plane[:], list1, U8, J, "xt_picked_scales", "picked_scales")
        w_rest_scales = keep.tile([P, PACK - 1, P], U8, name="w_rest_scales", tag="table_plane", align_bytes=64)
        nc.vector.tensor_copy(
            w_rest_scales[:].rearrange("p t m -> p m t"), w_plane[:].rearrange("p (m t) -> p m t", t=PACK)[:, :, 1:]
        )
        w_dealt_scales = [w_first_scales[:]] + [w_rest_scales[:, t, :] for t in range(PACK - 1)]
        a_sb = [keep.tile([P, J], F32, name="a_sb0")]
        for half in range(2):
            cols = slice(half * HALF, (half + 1) * HALF)
            a_ps = psum.tile([P, HALF], F32, name="a_half%d" % half, tag=("a_ps0", "b_ps3")[half])
            nc.tensor.matmul_mx(
                out=a_ps[:], lhsT=w_dealt[0][:].bitcast(FP8X4), lhsT_scale=w_dealt_scales[0],
                rhs=xt_picked[:, cols].bitcast(FP8X4), rhs_scale=xt_picked_scales[:, cols], start=True, stop=True,
            )
            if half == 0:
                nc.scalar.copy(a_sb[0][:, cols], a_ps[:])
            else:
                nc.vector.tensor_copy(a_sb[0][:, cols], a_ps[:])
        for t in range(1, PACK):
            a_ps = psum.tile([P, J], F32, name="a_ps%d" % t, tag="a_ps%d" % t)
            nc.tensor.matmul_mx(
                out=a_ps[:], lhsT=w_dealt[t][:].bitcast(FP8X4), lhsT_scale=w_dealt_scales[t],
                rhs=xt_picked[:].bitcast(FP8X4), rhs_scale=xt_picked_scales[:], start=True, stop=True,
            )
            a_t = keep.tile([P, J], F32, name="a_sb%d" % t, tag="a_sb%d" % t, align_bytes=64)
            nc.vector.tensor_copy(a_t[:], a_ps[:])
            a_sb.append(a_t)

        for t in range(2, PACK):
            board = keep.tile([P, C], F32, name="pw%d" % t, tag="w_dealt%d" % (t - 1), align_bytes=64)
            nc.vector.memset(board[:], 0.0)
            pw.append(board)

        xo_picked = gather(xo_all[:].bitcast(U32), list2, U32, J, "xo_picked", "picked_words")
        xo_picked_scales = gather(xo_plane[:], list2, U8, J, "xo_picked_scales", "picked_scales")
        w2_dealt = keep.tile([P, 2 * R], U8, name="w2_dealt", tag="w_dealt3", align_bytes=64)
        nc.vector.tensor_copy(
            w2_dealt[:].rearrange("p (t m b) -> p m t b", t=PACK, b=2),
            w2_raw[:].rearrange("p (m t b) -> p m t b", t=PACK, b=2),
        )
        w2_dealt_scales = keep.tile([P, PACK, P], U8, name="w2_dealt_scales", tag="table_plane", align_bytes=64)
        nc.vector.tensor_copy(
            w2_dealt_scales[:].rearrange("p t m -> p m t"), w2_plane[:].rearrange("p (m t) -> p m t", t=PACK)
        )
        b_ps = []
        for t in range(PACK):
            b_t = psum.tile([P, J], F32, name="b_ps%d" % t, tag="b_ps%d" % t)
            nc.tensor.matmul_mx(
                out=b_t[:], lhsT=w2_dealt[:, 2 * t * P : 2 * (t + 1) * P].bitcast(FP4X4), lhsT_scale=w2_dealt_scales[:, t, :],
                rhs=xo_picked[:].bitcast(FP8X4), rhs_scale=xo_picked_scales[:], start=True, stop=True,
            )
            b_ps.append(b_t)

        spent = ("xo_all", "w2_raw")
        pv = [keep.tile([P, C], F32, name="pv%d" % t, tag=spent[t], align_bytes=64) for t in range(2)]
        for board in pv:
            nc.vector.memset(board[:], 0.0)

        vs_all = load_words4(vs_words, U16, T, "vs_all", "table_words")
        vs_plane = zeroed_plane(T, "vs_plane", "w2_plane")
        load_scales(vs_plane, vs_scales, nc.sync)

        taken = keep.tile([P, PACK, J], F32, name="taken", tag="xo_plane", align_bytes=64)
        kept = [keep.tile([P, J], F32, name="kept%d" % t) for t in range(PACK)]

        def put_a(t):
            nc.scalar.activation(out=pw[t][:].indirect(list3[:]), in_=a_sb[t][:], func=COPY)

        def fetch_pw(t):
            nc.scalar.activation(out=taken[:, t, :], in_=pw[t][:].indirect(list4[:]), func=COPY, scale=sa_sb[:, t : t + 1])
            h1 = keep.tile([P, J], F32, name="h1_%d" % t, tag="h1_%d" % t, align_bytes=64)
            nc.vector.tensor_tensor(h1[:], b_ps[t][:], taken[:, t, :], SUB)
            nc.vector.tensor_scalar_max(kept[t][:], h1[:], 0.0)

        def put_h(t):
            nc.scalar.activation(out=pv[t][:].indirect(list5[:]), in_=kept[t][:], func=COPY)

        def fetch_g(t):
            nc.scalar.activation(out=hid[:, t, :], in_=pv[t][:].indirect(list6[:]), func=COPY, scale=sb_sb[:, t : t + 1])

        for half in range(2):
            nc.scalar.activation(
                out=pw[0][:].indirect(list3[:, half * HALF // 16 : (half + 1) * HALF // 16]),
                in_=a_sb[0][:, half * HALF : (half + 1) * HALF], func=COPY,
            )
        for t in range(1, PACK):
            put_a(t)
        for t in range(PACK):
            fetch_pw(t)
        for t in range(2, PACK):
            board = keep.tile([P, C], F32, name="pv%d" % t, tag="pw%d" % (t - 2))
            nc.vector.memset(board[:], 0.0)
            pv.append(board)
        vs_picked = gather(vs_all[:], list7, U16, N, "vs_picked", "h1_0")
        vs_picked_scales = gather(vs_plane[:], list7, U8, N, "vs_picked_scales", "h1_1")
        for t in range(PACK):
            put_h(t)
        hid = keep.tile([P, PACK, O], BF16, name="hid", tag="h1_%d" % (PACK - 1), align_bytes=64)
        for t in range(PACK):
            fetch_g(t)

        woven = keep.tile([P, O, PACK], BF16, name="woven", align_bytes=64)
        nc.vector.tensor_copy(
            woven[:].rearrange("p (c i) t -> p c t i", i=4),
            hid[:].rearrange("p t (c i) -> p c t i", i=4),
        )
        hid_codes = keep.tile([P, O], U32, name="hid_codes", align_bytes=64)
        hid_scales = keep.tile([P, O], U8, name="hid_scales", align_bytes=64)
        nc.vector.quantize_mx(
            out=hid_codes[:].bitcast(FP8X4), scales=hid_scales[:], in_=woven[:].rearrange("p o t -> p (o t)"),
        )
        for half in range(N // P):
            y_ps = psum.tile([P, O], F32, name="y_ps%d" % half, tag="a_ps%d" % half)
            nc.tensor.matmul_mx(
                out=y_ps[:], lhsT=vs_picked[:, half * P : (half + 1) * P].bitcast(FP4X4),
                lhsT_scale=vs_picked_scales[:, half * P : (half + 1) * P],
                rhs=hid_codes[:].bitcast(FP8X4), rhs_scale=hid_scales[:], start=True, stop=True,
            )
            y_sb = keep.tile([P, O], F32, name="y_sb%d" % half)
            if half == 0:
                nc.vector.tensor_copy(y_sb[:], y_ps[:])
                nc.sync.dma_start(out[half * P : (half + 1) * P, :], y_sb[:])
            else:
                nc.scalar.copy(y_sb[:], y_ps[:])
                nc.scalar.dma_start(out[half * P : (half + 1) * P, :], y_sb[:])
